import numpy as np
import ml_dtypes


def mxq(x, axis, fmt="e4m3"):
    dtype, down = {"e4m3": (ml_dtypes.float8_e4m3fn, 7), "e5m2": (ml_dtypes.float8_e5m2, 14)}[fmt]
    v = np.moveaxis(np.asarray(x, np.float32).astype(ml_dtypes.bfloat16).astype(np.float64), axis, -1)
    blocks = v.reshape(v.shape[:-1] + (-1, 32))
    amax = np.abs(blocks).max(-1, keepdims=True)
    byte = np.maximum(np.where(amax > 0, np.frexp(amax)[1] - 1 + 127, 0) - down, 1)
    scale = np.exp2(byte - 127.0)
    codes = (blocks / scale).astype(np.float32).astype(dtype).astype(np.float64)
    return np.moveaxis((codes * scale).reshape(v.shape), -1, axis)


WIDE = False


def mx_kscale(k):
    if not WIDE:
        return np.ones(k)
    levels = np.array([10, -10, 5, -5, 0])
    if k % 512:
        return np.exp2(np.random.permutation(np.resize(levels, k // 32))).repeat(32)
    a = np.empty((k // 512, 16))
    for p in range(k // 512):
        a[p, :8] = np.random.permutation(np.resize(levels, 8))
        for g in range(8):
            far = levels[np.abs(levels - a[p, g]) >= 10]
            a[p, g + 8] = far[np.random.randint(len(far))]
    return np.exp2(a.ravel()).repeat(32)


def f64(x):
    return np.asarray(x).astype(np.float64)


E2M1 = np.array([0.0, 0.5, 1.0, 1.5, 2.0, 3.0, 4.0, 6.0, -0.0, -0.5, -1.0, -1.5, -2.0, -3.0, -4.0, -6.0])


def pack_weight(w, fmt):
    k, n = w.shape
    w = f64(np.asarray(w, np.float32).astype(ml_dtypes.bfloat16)).reshape(k // 32, 32, n)
    amax = np.abs(w).max(1)
    if fmt == "e4m3":
        byte = np.frexp(amax)[1] - 1 + 127 - 7
    else:
        mant, ex = np.frexp(amax / 6.0)
        byte = np.where(mant > 0.5, ex, ex - 1) + 127
    byte = np.clip(np.where(amax > 0, byte, 1), 1, 254)
    scaled = (w * np.exp2(127.0 - byte)[:, None, :]).reshape(k, n).astype(np.float32)
    by_word = np.ascontiguousarray(scaled.reshape(k // 512, 128, 4, n).transpose(0, 1, 3, 2))
    if fmt == "e4m3":
        words = by_word.astype(ml_dtypes.float8_e4m3fn).view(np.uint8)
    else:
        c = by_word.astype(ml_dtypes.float4_e2m1fn).view(np.uint8) & 0xF
        words = (c[..., 0::2] | (c[..., 1::2] << 4)).reshape(k // 512, 128, 2 * n)
    return np.ascontiguousarray(words), np.ascontiguousarray(byte.astype(np.uint8).reshape(k // 512, 16, n))


def unpack_weight(words, scales, fmt):
    g, _, n = scales.shape
    words = np.ascontiguousarray(words).reshape(g, 128, n, -1)
    if fmt == "e4m3":
        vals = words.view(ml_dtypes.float8_e4m3fn).astype(np.float64)
    else:
        nib = np.empty((g, 128, n, 4), np.uint8)
        nib[..., 0::2] = words & 0xF
        nib[..., 1::2] = words >> 4
        vals = E2M1[nib]
    vals = vals * np.repeat(np.exp2(scales.astype(np.float64) - 127.0), 8, axis=1)[..., None]
    return vals.transpose(0, 1, 3, 2).reshape(g * 512, n)


K, L, T, R, N = 1024, 1024, 512, 512, 512


def setup_inputs():
    n = np.random.standard_normal
    fk = mx_kscale(K)
    fr = mx_kscale(R)
    fl = mx_kscale(L)
    xtp = pack_weight(n((K, T)) / fk[:, None], "e4m3")
    wap = pack_weight(n((K, R)) * 1 / np.sqrt(K) * fk[:, None] * fr, "e2m1")
    wbp = pack_weight(n((R, N)) * 1 / np.sqrt(R) / fr[:, None], "e4m3")
    xqp = pack_weight(n((L, T)) / fl[:, None], "e2m1")
    wqp = pack_weight(n((L, N)) * 1 / np.sqrt(L) * fl[:, None], "e4m3")
    return {
        "xt_words": xtp[0],
        "xt_scales": xtp[1],
        "wa_words": wap[0],
        "wa_scales": wap[1],
        "wb_words": wbp[0],
        "wb_scales": wbp[1],
        "xq_words": xqp[0],
        "xq_scales": xqp[1],
        "wq_words": wqp[0],
        "wq_scales": wqp[1],
        "tg": (1.0 * n((N, T))).astype(np.float32),
    }


def reference(xt_words, xt_scales, wa_words, wa_scales, wb_words, wb_scales, xq_words, xq_scales, wq_words, wq_scales, tg):
    xtu = unpack_weight(xt_words, xt_scales, "e4m3")
    wau = unpack_weight(wa_words, wa_scales, "e2m1")
    wbu = unpack_weight(wb_words, wb_scales, "e4m3")
    xqu = unpack_weight(xq_words, xq_scales, "e2m1")
    wqu = unpack_weight(wq_words, wq_scales, "e4m3")
    a = wau.T @ xtu
    hid = np.maximum(a, 0.0)
    hidq = mxq(hid, 0, "e4m3")
    p = wbu.T @ hidq + wqu.T @ xqu
    y = np.tanh(f64(tg) - p)
    return y

@@ -1,0 +1,160 @@
+from contextlib import ExitStack
+
+import concourse.mybir as mybir
+from concourse.masks import make_identity
+
+K, L, T, R, N = 1024, 1024, 512, 512, 512
+FLOPS = 2 * T * (K * R + R * N + L * N)
+
+F32 = mybir.dt.float32
+BF16 = mybir.dt.bfloat16
+I32 = mybir.dt.int32
+U32 = mybir.dt.uint32
+U8 = mybir.dt.uint8
+FP8X4 = mybir.dt.float8_e4m3fn_x4
+FP4X4 = mybir.dt.float4_e2m1fn_x4
+ACT = mybir.ActivationFunctionType
+ALU = mybir.AluOpType
+
+P = 128
+CHUNKS = T // P
+N_TILES = N // P
+WARM_PASSES = 18
+
+
+def tile_mix_unexplained_rest_kernel(tc, xt_words, xt_scales, wa_words, wa_scales, wb_words, wb_scales,
+                                           xq_words, xq_scales, wq_words, wq_scales, tg, out):
+    nc = tc.nc
+    with ExitStack() as ctx:
+        sb = ctx.enter_context(tc.tile_pool(name="sb", bufs=1))
+        ps = ctx.enter_context(tc.psum_pool(name="ps", bufs=1))
+        ctx.enter_context(tc.manual_schedule())
+
+        def stage_scales(staged, first, scales):
+            passes = scales.shape[0]
+            nc.sync.dma_start(out=staged[4:P:8, first:first + passes, :].bitcast(I32),
+                              in_=scales.rearrange("z q c -> q z c").bitcast(I32))
+
+        def spread_scales(planes, staged):
+            for r in range(4):
+                nc.sync.dma_start(out=planes[r:P:32, :, :].rearrange("q z c -> q (z c)").bitcast(I32),
+                                  in_=staged[8 * r + 4:P:32, :, :].rearrange("q z c -> q (z c)").bitcast(I32))
+
+        def load_words(name, words, dtype):
+            tile = sb.tile(list(words.shape[:2]) + [words.shape[2] // (4 if dtype == U32 else 1)], dtype, name=name,
+                           align_bytes=64)
+            nc.sync.dma_start(out=tile[:].bitcast(I32), in_=words.bitcast(I32))
+            return tile
+
+        warm_in = sb.tile([P, 512], BF16, name="warm_in", align_bytes=64)
+        nc.gpsimd.memset(warm_in[:].bitcast(I32), 0)
+        warm_c = sb.tile([P, P], U32, name="warm_c", align_bytes=64)
+        warm_s = sb.tile([P, P], U8, name="warm_s", align_bytes=64)
+        nc.vector.quantize_mx(out=warm_c[:].bitcast(FP8X4), scales=warm_s[:], in_=warm_in[:])
+        table_probe = sb.tile([P, 1], F32, name="table_probe")
+        nc.scalar.activation(out=table_probe[:], in_=warm_in[:, 0:1], func=ACT.Tanh)
+
+        planes1 = sb.tile([P, 4, 512], U8, name="planes1", align_bytes=64)
+        planes2 = sb.tile([P, 5, 512], U8, name="planes2", align_bytes=64)
+        for planes in (planes1, planes2):
+            nc.vector.memset(planes[:].rearrange("p z c -> p (z c)").bitcast(I32), 0)
+        xt_s, wa_s = planes1[:, 0:2, :], planes1[:, 2:4, :]
+        xq_s, wq_s, wb_s = planes2[:, 0:2, :], planes2[:, 2:4, :], planes2[:, 4:5, :]
+
+        ident = sb.tile([P, P], F32, name="ident")
+        make_identity(nc, ident[:])
+
+        staged1 = sb.tile([P, 4, 512], U8, name="staged1", align_bytes=64)
+        staged2 = sb.tile([P, 5, 512], U8, name="staged2", align_bytes=64)
+        xt_v = xt_words.rearrange("z p n t -> p z (n t)")
+        stage_scales(staged1, 0, xt_scales)
+        stage_scales(staged1, 2, wa_scales)
+        stage_scales(staged2, 0, xq_scales)
+        stage_scales(staged2, 2, wq_scales)
+        stage_scales(staged2, 4, wb_scales)
+        wa_c = load_words("wa_c", wa_words.rearrange("z p b -> p z b"), U8)
+        xt_c = [load_words("xt_c0", xt_v[:, :, 0:1024], U32)]
+        spread_scales(planes1, staged1)
+        xt_c.append(load_words("xt_c1", xt_v[:, :, 1024:2048], U32))
+        xq_c = load_words("xq_c", xq_words.rearrange("z p b -> p z b"), U8)
+        wq_c = load_words("wq_c", wq_words.rearrange("z p n t -> p z (n t)"), U32)
+        wb_c = load_words("wb_c", wb_words.rearrange("z p n t -> p z (n t)"), U32)
+        spread_scales(planes2, staged2)
+        tg_t = []
+        for h in range(2):
+            pair = sb.tile([P, 2, T], F32, name="tg%d" % h)
+            nc.sync.dma_start(out=pair[:], in_=tg[2 * h * P:(2 * h + 2) * P, :].rearrange("(i p) t -> p i t", p=P))
+            tg_t.extend([pair[:, 0, :], pair[:, 1, :]])
+
+        warm_out = ps.tile([P, P], F32, name="warm_out", tag="sum3")
+        for w in range(WARM_PASSES):
+            nc.tensor.matmul_mx(out=warm_out[:], lhsT=warm_c[:].bitcast(FP8X4), lhsT_scale=warm_s[:],
+                                rhs=warm_c[:].bitcast(FP8X4), rhs_scale=warm_s[:], start=True, stop=True)
+
+        hid_rows = []
+        for c in range(CHUNKS):
+            a_t = ps.tile([P, R], F32, name="a_t%d" % c, tag="chunk%d" % c)
+            cols = slice((c % 2) * P, (c % 2 + 1) * P)
+            for z in range(2):
+                nc.tensor.matmul_mx(out=a_t[:], lhsT=xt_c[c // 2][:, z, cols].bitcast(FP8X4),
+                                    lhsT_scale=xt_s[:, z, c * P:(c + 1) * P],
+                                    rhs=wa_c[:, z, :].bitcast(FP4X4), rhs_scale=wa_s[:, z, :],
+                                    start=(z == 0), stop=(z == 1))
+            rows = sb.tile([P, R], BF16, name="hid_rows%d" % c, align_bytes=64)
+            src = a_t[:].rearrange("t (p u e) -> t u p e", u=2, e=2)
+            dst = rows[:].rearrange("t (u p e) -> t u p e", u=2, e=2)
+            if c % 2 == 0:
+                nc.scalar.activation(out=dst, in_=src, func=ACT.Relu)
+            else:
+                nc.vector.tensor_scalar(out=dst, in0=src, scalar1=0.0, scalar2=None, op0=ALU.max)
+            hid_rows.append(rows)
+
+        hid_in = [sb.tile([P, 2 * P * 4], BF16, name="hid_in%d" % h, align_bytes=64) for h in range(2)]
+        for c in range(CHUNKS):
+            turned = ps.tile([P, 2, P], F32, name="turned%d" % c, tag="chunk%d" % c)
+            words = hid_rows[c][:].bitcast(F32)
+            for u in range(2):
+                nc.tensor.transpose(turned[:, u, :], words[:, u * P:(u + 1) * P], ident[:])
+            dst = hid_in[c // 2][:].bitcast(F32)[:, (c % 2) * 2 * P:(c % 2 + 1) * 2 * P].rearrange("p (t u) -> p t u", u=2)
+            src = turned[:].rearrange("p u t -> p t u")
+            if c == 2:
+                nc.vector.tensor_copy(out=dst, in_=src)
+            else:
+                nc.scalar.copy(out=dst, in_=src)
+
+        hid_c = sb.tile([P, T], U32, name="hid_c", align_bytes=64)
+        hid_s = sb.tile([P, T], U8, name="hid_s", align_bytes=64)
+        for h in range(2):
+            cols = slice(h * 2 * P, (h + 1) * 2 * P)
+            nc.vector.quantize_mx(out=hid_c[:, cols].bitcast(FP8X4), scales=hid_s[:, cols], in_=hid_in[h][:])
+
+        sums = [ps.tile([P, T], F32, name="sum%d" % i, tag="sum%d" % i) for i in range(N_TILES)]
+
+        def second_input_passes(i):
+            for z in range(2):
+                nc.tensor.matmul_mx(out=sums[i][:], lhsT=wq_c[:, z, i * P:(i + 1) * P].bitcast(FP8X4),
+                                    lhsT_scale=wq_s[:, z, i * P:(i + 1) * P],
+                                    rhs=xq_c[:, z, :].bitcast(FP4X4), rhs_scale=xq_s[:, z, :],
+                                    start=(z == 0), stop=False)
+
+        def hidden_pass_and_finish(i, pieces):
+            nc.tensor.matmul_mx(out=sums[i][:], lhsT=wb_c[:, 0, i * P:(i + 1) * P].bitcast(FP8X4),
+                                lhsT_scale=wb_s[:, 0, i * P:(i + 1) * P],
+                                rhs=hid_c[:].bitcast(FP8X4), rhs_scale=hid_s[:], start=False, stop=True)
+            width = T // pieces
+            for j in range(pieces):
+                cols = slice(j * width, (j + 1) * width)
+                rest = sb.tile([P, width], F32, name="rest%d_%d" % (i, j))
+                nc.vector.tensor_tensor(out=rest[:], in0=tg_t[i][:, cols], in1=sums[i][:, cols], op=ALU.subtract)
+                result = sb.tile([P, width], F32, name="result%d_%d" % (i, j))
+                nc.scalar.activation(out=result[:], in_=rest[:], func=ACT.Tanh)
+                nc.sync.dma_start(out=out[i * P:(i + 1) * P, cols], in_=result[:])
+
+        second_input_passes(0)
+        second_input_passes(1)
+        hidden_pass_and_finish(0, 1)
+        hidden_pass_and_finish(1, 1)
+        second_input_passes(2)
+        hidden_pass_and_finish(2, 1)
+        second_input_passes(3)
+        hidden_pass_and_finish(3, 2)

@@ -1,7 +1,6 @@
 from contextlib import ExitStack
 
 import concourse.mybir as mybir
-from concourse.masks import make_identity
 
 K, L, T, R, N = 1024, 1024, 512, 512, 512
 FLOPS = 2 * T * (K * R + R * N + L * N)
@@ -18,8 +17,8 @@ ALU = mybir.AluOpType
 
 P = 128
 CHUNKS = T // P
-N_TILES = N // P
-WARM_PASSES = 18
+HALF = T // 2
+WARM_PASSES = 28
 
 
 def tile_mix_unexplained_rest_kernel(tc, xt_words, xt_scales, wa_words, wa_scales, wb_words, wb_scales,
@@ -46,115 +45,133 @@ def tile_mix_unexplained_rest_kernel(tc, xt_words, xt_scales, wa_words, wa_scale
             nc.sync.dma_start(out=tile[:].bitcast(I32), in_=words.bitcast(I32))
             return tile
 
+        wa_s_raw = sb.tile([P, 2, R], U8, name="wa_s_raw", align_bytes=64)
+        nc.gpsimd.memset(wa_s_raw[:].rearrange("p z c -> p (z c)").bitcast(I32), 0)
         warm_in = sb.tile([P, 512], BF16, name="warm_in", align_bytes=64)
-        nc.gpsimd.memset(warm_in[:].bitcast(I32), 0)
+        nc.vector.memset(warm_in[:].bitcast(I32), 0)
+        xt_s = sb.tile([P, 2, 512], U8, name="xt_s", align_bytes=64)
+        nc.vector.memset(xt_s[:].rearrange("p z c -> p (z c)").bitcast(I32), 0)
         warm_c = sb.tile([P, P], U32, name="warm_c", align_bytes=64)
         warm_s = sb.tile([P, P], U8, name="warm_s", align_bytes=64)
         nc.vector.quantize_mx(out=warm_c[:].bitcast(FP8X4), scales=warm_s[:], in_=warm_in[:])
         table_probe = sb.tile([P, 1], F32, name="table_probe")
         nc.scalar.activation(out=table_probe[:], in_=warm_in[:, 0:1], func=ACT.Tanh)
-
-        planes1 = sb.tile([P, 4, 512], U8, name="planes1", align_bytes=64)
         planes2 = sb.tile([P, 5, 512], U8, name="planes2", align_bytes=64)
-        for planes in (planes1, planes2):
-            nc.vector.memset(planes[:].rearrange("p z c -> p (z c)").bitcast(I32), 0)
-        xt_s, wa_s = planes1[:, 0:2, :], planes1[:, 2:4, :]
+        nc.vector.memset(planes2[:].rearrange("p z c -> p (z c)").bitcast(I32), 0)
         xq_s, wq_s, wb_s = planes2[:, 0:2, :], planes2[:, 2:4, :], planes2[:, 4:5, :]
 
-        ident = sb.tile([P, P], F32, name="ident")
-        make_identity(nc, ident[:])
+        def load_scale_rows(plane, scales, r):
+            nc.sync.dma_start(out=plane[r:P:32, :, :].bitcast(I32),
+                              in_=scales.rearrange("z (q r) c -> r q z c", r=4)[r].bitcast(I32))
 
-        staged1 = sb.tile([P, 4, 512], U8, name="staged1", align_bytes=64)
         staged2 = sb.tile([P, 5, 512], U8, name="staged2", align_bytes=64)
-        xt_v = xt_words.rearrange("z p n t -> p z (n t)")
-        stage_scales(staged1, 0, xt_scales)
-        stage_scales(staged1, 2, wa_scales)
+        wa_raw = load_words("wa_raw", wa_words.rearrange("z p b -> p z b"), U8)
+        for r in range(4):
+            load_scale_rows(wa_s_raw, wa_scales, r)
+        for r in range(2):
+            load_scale_rows(xt_s, xt_scales, r)
+        xt_c = load_words("xt_c", xt_words.rearrange("z p n t -> p z (n t)"), U32)
+        for r in range(2, 4):
+            load_scale_rows(xt_s, xt_scales, r)
         stage_scales(staged2, 0, xq_scales)
         stage_scales(staged2, 2, wq_scales)
         stage_scales(staged2, 4, wb_scales)
-        wa_c = load_words("wa_c", wa_words.rearrange("z p b -> p z b"), U8)
-        xt_c = [load_words("xt_c0", xt_v[:, :, 0:1024], U32)]
-        spread_scales(planes1, staged1)
-        xt_c.append(load_words("xt_c1", xt_v[:, :, 1024:2048], U32))
-        xq_c = load_words("xq_c", xq_words.rearrange("z p b -> p z b"), U8)
         wq_c = load_words("wq_c", wq_words.rearrange("z p n t -> p z (n t)"), U32)
-        wb_c = load_words("wb_c", wb_words.rearrange("z p n t -> p z (n t)"), U32)
+        xq_c = load_words("xq_c", xq_words.rearrange("z p b -> p z b"), U8)
         spread_scales(planes2, staged2)
-        tg_t = []
+        wb_c = load_words("wb_c", wb_words.rearrange("z p n t -> p z (n t)"), U32)
+        tg_t = {}
         for h in range(2):
-            pair = sb.tile([P, 2, T], F32, name="tg%d" % h)
-            nc.sync.dma_start(out=pair[:], in_=tg[2 * h * P:(2 * h + 2) * P, :].rearrange("(i p) t -> p i t", p=P))
-            tg_t.extend([pair[:, 0, :], pair[:, 1, :]])
+            for pair in range(2):
+                part = sb.tile([P, 2, HALF], F32, name="tg%d_%d" % (h, pair))
+                nc.sync.dma_start(out=part[:], in_=tg[2 * pair * P:(2 * pair + 2) * P, h * HALF:(h + 1) * HALF]
+                                  .rearrange("(i p) t -> p i t", p=P))
+                tg_t[(h, 2 * pair)] = part[:, 0, :]
+                tg_t[(h, 2 * pair + 1)] = part[:, 1, :]
+
+        wa_s = sb.tile([P, 2, R], U8, name="wa_s", align_bytes=64)
+        wa_c = [sb.tile([P, 2 * R], U8, name="wa_c%d" % z, align_bytes=64) for z in range(2)]
+
+        def gather_code_columns(z):
+            nc.vector.tensor_copy(out=wa_c[z][:].rearrange("p (j m b) -> p j m b", j=4, b=2),
+                                  in_=wa_raw[:, z, :].rearrange("p (m j b) -> p j m b", j=4, b=2))
+
+        gather_code_columns(0)
+        nc.vector.tensor_copy(out=wa_s[:].rearrange("p z (j m) -> p z j m", j=4),
+                              in_=wa_s_raw[:].rearrange("p z (m j) -> p z j m", j=4))
+        gather_code_columns(1)
 
         warm_out = ps.tile([P, P], F32, name="warm_out", tag="sum3")
         for w in range(WARM_PASSES):
             nc.tensor.matmul_mx(out=warm_out[:], lhsT=warm_c[:].bitcast(FP8X4), lhsT_scale=warm_s[:],
                                 rhs=warm_c[:].bitcast(FP8X4), rhs_scale=warm_s[:], start=True, stop=True)
 
-        hid_rows = []
-        for c in range(CHUNKS):
-            a_t = ps.tile([P, R], F32, name="a_t%d" % c, tag="chunk%d" % c)
-            cols = slice((c % 2) * P, (c % 2 + 1) * P)
-            for z in range(2):
-                nc.tensor.matmul_mx(out=a_t[:], lhsT=xt_c[c // 2][:, z, cols].bitcast(FP8X4),
-                                    lhsT_scale=xt_s[:, z, c * P:(c + 1) * P],
-                                    rhs=wa_c[:, z, :].bitcast(FP4X4), rhs_scale=wa_s[:, z, :],
-                                    start=(z == 0), stop=(z == 1))
-            rows = sb.tile([P, R], BF16, name="hid_rows%d" % c, align_bytes=64)
-            src = a_t[:].rearrange("t (p u e) -> t u p e", u=2, e=2)
-            dst = rows[:].rearrange("t (u p e) -> t u p e", u=2, e=2)
+        hid_c = sb.tile([P, T], U32, name="hid_c", align_bytes=64)
+        hid_s = sb.tile([P, T], U8, name="hid_s", align_bytes=64)
+        pre = [ps.tile([P, 4, P], F32, name="pre%d" % c, tag="chunk%d" % c) for c in range(CHUNKS)]
+        hid_in = [sb.tile([P, P * 4], BF16, name="hid_in%d" % c, align_bytes=64) for c in range(CHUNKS)]
+
+        def first_layer_pass(c, z):
+            cols = slice(c * P, (c + 1) * P)
+            for j in range(4):
+                nc.tensor.matmul_mx(out=pre[c][:, j, :], lhsT=wa_c[z][:, j * 2 * P:(j + 1) * 2 * P].bitcast(FP4X4),
+                                    lhsT_scale=wa_s[:, z, j * P:(j + 1) * P],
+                                    rhs=xt_c[:, z, cols].bitcast(FP8X4),
+                                    rhs_scale=xt_s[:, z, cols],
+                                    start=(z == 0 and j == 0), stop=(z == 1 and j == 3))
+
+        def relu_out(c):
+            src = pre[c][:].rearrange("p j t -> p t j")
+            dst = hid_in[c][:].rearrange("p (t j) -> p t j", j=4)
             if c % 2 == 0:
                 nc.scalar.activation(out=dst, in_=src, func=ACT.Relu)
             else:
                 nc.vector.tensor_scalar(out=dst, in0=src, scalar1=0.0, scalar2=None, op0=ALU.max)
-            hid_rows.append(rows)
 
-        hid_in = [sb.tile([P, 2 * P * 4], BF16, name="hid_in%d" % h, align_bytes=64) for h in range(2)]
-        for c in range(CHUNKS):
-            turned = ps.tile([P, 2, P], F32, name="turned%d" % c, tag="chunk%d" % c)
-            words = hid_rows[c][:].bitcast(F32)
-            for u in range(2):
-                nc.tensor.transpose(turned[:, u, :], words[:, u * P:(u + 1) * P], ident[:])
-            dst = hid_in[c // 2][:].bitcast(F32)[:, (c % 2) * 2 * P:(c % 2 + 1) * 2 * P].rearrange("p (t u) -> p t u", u=2)
-            src = turned[:].rearrange("p u t -> p t u")
-            if c == 2:
-                nc.vector.tensor_copy(out=dst, in_=src)
-            else:
-                nc.scalar.copy(out=dst, in_=src)
+        def quantize_chunk(c):
+            cols = slice(c * P, (c + 1) * P)
+            nc.vector.quantize_mx(out=hid_c[:, cols].bitcast(FP8X4), scales=hid_s[:, cols], in_=hid_in[c][:])
 
-        hid_c = sb.tile([P, T], U32, name="hid_c", align_bytes=64)
-        hid_s = sb.tile([P, T], U8, name="hid_s", align_bytes=64)
-        for h in range(2):
-            cols = slice(h * 2 * P, (h + 1) * 2 * P)
-            nc.vector.quantize_mx(out=hid_c[:, cols].bitcast(FP8X4), scales=hid_s[:, cols], in_=hid_in[h][:])
-
-        sums = [ps.tile([P, T], F32, name="sum%d" % i, tag="sum%d" % i) for i in range(N_TILES)]
-
-        def second_input_passes(i):
+        for first in (0, 2):
             for z in range(2):
-                nc.tensor.matmul_mx(out=sums[i][:], lhsT=wq_c[:, z, i * P:(i + 1) * P].bitcast(FP8X4),
-                                    lhsT_scale=wq_s[:, z, i * P:(i + 1) * P],
-                                    rhs=xq_c[:, z, :].bitcast(FP4X4), rhs_scale=xq_s[:, z, :],
-                                    start=(z == 0), stop=False)
+                first_layer_pass(first, z)
+                first_layer_pass(first + 1, z)
+            relu_out(first)
+            relu_out(first + 1)
+            quantize_chunk(first)
+            quantize_chunk(first + 1)
 
-        def hidden_pass_and_finish(i, pieces):
-            nc.tensor.matmul_mx(out=sums[i][:], lhsT=wb_c[:, 0, i * P:(i + 1) * P].bitcast(FP8X4),
-                                lhsT_scale=wb_s[:, 0, i * P:(i + 1) * P],
-                                rhs=hid_c[:].bitcast(FP8X4), rhs_scale=hid_s[:], start=False, stop=True)
-            width = T // pieces
-            for j in range(pieces):
-                cols = slice(j * width, (j + 1) * width)
-                rest = sb.tile([P, width], F32, name="rest%d_%d" % (i, j))
-                nc.vector.tensor_tensor(out=rest[:], in0=tg_t[i][:, cols], in1=sums[i][:, cols], op=ALU.subtract)
-                result = sb.tile([P, width], F32, name="result%d_%d" % (i, j))
-                nc.scalar.activation(out=result[:], in_=rest[:], func=ACT.Tanh)
-                nc.sync.dma_start(out=out[i * P:(i + 1) * P, cols], in_=result[:])
+        pieces = [(i, 0, HALF) for i in range(4)] + [(i, HALF, T) for i in range(3)]
+        pieces = pieces + [(3, HALF, HALF + P), (3, HALF + P, T)]
+        banks = ["sum%d" % i for i in range(4)] + ["chunk%d" % c for c in range(CHUNKS)]
 
-        second_input_passes(0)
-        second_input_passes(1)
-        hidden_pass_and_finish(0, 1)
-        hidden_pass_and_finish(1, 1)
-        second_input_passes(2)
-        hidden_pass_and_finish(2, 1)
-        second_input_passes(3)
-        hidden_pass_and_finish(3, 2)
+        def second_input_passes(k):
+            i, t0, t1 = pieces[k]
+            rows = slice(i * P, (i + 1) * P)
+            total = ps.tile([P, t1 - t0], F32, name="total%d" % k, tag=banks[k % len(banks)])
+            for z in range(2):
+                for c0 in range(t0, t1, P):
+                    nc.tensor.matmul_mx(out=total[:, c0 - t0:c0 - t0 + P], lhsT=wq_c[:, z, rows].bitcast(FP8X4),
+                                        lhsT_scale=wq_s[:, z, rows],
+                                        rhs=xq_c[:, z, 2 * c0:2 * (c0 + P)].bitcast(FP4X4),
+                                        rhs_scale=xq_s[:, z, c0:c0 + P], start=(z == 0 and c0 == t0), stop=False)
+            return total
+
+        def finish(k, total):
+            i, t0, t1 = pieces[k]
+            rows = slice(i * P, (i + 1) * P)
+            nc.tensor.matmul_mx(out=total[:], lhsT=wb_c[:, 0, rows].bitcast(FP8X4), lhsT_scale=wb_s[:, 0, rows],
+                                rhs=hid_c[:, t0:t1].bitcast(FP8X4), rhs_scale=hid_s[:, t0:t1], start=False, stop=True)
+            h = t0 // HALF
+            rest = sb.tile([P, t1 - t0], F32, name="rest%d" % k)
+            nc.vector.tensor_tensor(out=rest[:], in0=tg_t[(h, i)][:, t0 - h * HALF:t1 - h * HALF], in1=total[:],
+                                    op=ALU.subtract)
+            result = sb.tile([P, t1 - t0], F32, name="result%d" % k)
+            nc.scalar.activation(out=result[:], in_=rest[:], func=ACT.Tanh)
+            nc.sync.dma_start(out=out[rows, t0:t1], in_=result[:])
+
+        leading = [second_input_passes(0), second_input_passes(1)]
+        finish(0, leading[0])
+        finish(1, leading[1])
+        for k in range(2, len(pieces)):
+            finish(k, second_input_passes(k))

@@ -18,7 +18,6 @@ ALU = mybir.AluOpType
 P = 128
 CHUNKS = T // P
 HALF = T // 2
-WARM_PASSES = 28
 
 
 def tile_mix_unexplained_rest_kernel(tc, xt_words, xt_scales, wa_words, wa_scales, wb_words, wb_scales,
@@ -47,15 +46,12 @@ def tile_mix_unexplained_rest_kernel(tc, xt_words, xt_scales, wa_words, wa_scale
 
         wa_s_raw = sb.tile([P, 2, R], U8, name="wa_s_raw", align_bytes=64)
         nc.gpsimd.memset(wa_s_raw[:].rearrange("p z c -> p (z c)").bitcast(I32), 0)
-        warm_in = sb.tile([P, 512], BF16, name="warm_in", align_bytes=64)
-        nc.vector.memset(warm_in[:].bitcast(I32), 0)
         xt_s = sb.tile([P, 2, 512], U8, name="xt_s", align_bytes=64)
         nc.vector.memset(xt_s[:].rearrange("p z c -> p (z c)").bitcast(I32), 0)
-        warm_c = sb.tile([P, P], U32, name="warm_c", align_bytes=64)
-        warm_s = sb.tile([P, P], U8, name="warm_s", align_bytes=64)
-        nc.vector.quantize_mx(out=warm_c[:].bitcast(FP8X4), scales=warm_s[:], in_=warm_in[:])
+        probe_in = sb.tile([P, 1], F32, name="probe_in")
+        nc.vector.memset(probe_in[:], 0.0)
         table_probe = sb.tile([P, 1], F32, name="table_probe")
-        nc.scalar.activation(out=table_probe[:], in_=warm_in[:, 0:1], func=ACT.Tanh)
+        nc.scalar.activation(out=table_probe[:], in_=probe_in[:], func=ACT.Tanh)
         planes2 = sb.tile([P, 5, 512], U8, name="planes2", align_bytes=64)
         nc.vector.memset(planes2[:].rearrange("p z c -> p (z c)").bitcast(I32), 0)
         xq_s, wq_s, wb_s = planes2[:, 0:2, :], planes2[:, 2:4, :], planes2[:, 4:5, :]
@@ -100,11 +96,6 @@ def tile_mix_unexplained_rest_kernel(tc, xt_words, xt_scales, wa_words, wa_scale
         nc.vector.tensor_copy(out=wa_s[:].rearrange("p z (j m) -> p z j m", j=4),
                               in_=wa_s_raw[:].rearrange("p z (m j) -> p z j m", j=4))
         gather_code_columns(1)
-
-        warm_out = ps.tile([P, P], F32, name="warm_out", tag="sum3")
-        for w in range(WARM_PASSES):
-            nc.tensor.matmul_mx(out=warm_out[:], lhsT=warm_c[:].bitcast(FP8X4), lhsT_scale=warm_s[:],
-                                rhs=warm_c[:].bitcast(FP8X4), rhs_scale=warm_s[:], start=True, stop=True)
 
         hid_c = sb.tile([P, T], U32, name="hid_c", align_bytes=64)
         hid_s = sb.tile([P, T], U8, name="hid_s", align_bytes=64)

from contextlib import ExitStack

import concourse.mybir as mybir

K, L, T, R, N = 1024, 1024, 512, 512, 512
FLOPS = 2 * T * (K * R + R * N + L * N)

F32 = mybir.dt.float32
BF16 = mybir.dt.bfloat16
I32 = mybir.dt.int32
U32 = mybir.dt.uint32
U8 = mybir.dt.uint8
FP8X4 = mybir.dt.float8_e4m3fn_x4
FP4X4 = mybir.dt.float4_e2m1fn_x4
ACT = mybir.ActivationFunctionType
ALU = mybir.AluOpType

P = 128
CHUNKS = T // P
HALF = T // 2


def tile_mix_unexplained_rest_kernel(tc, xt_words, xt_scales, wa_words, wa_scales, wb_words, wb_scales,
                                           xq_words, xq_scales, wq_words, wq_scales, tg, out):
    nc = tc.nc
    with ExitStack() as ctx:
        sb = ctx.enter_context(tc.tile_pool(name="sb", bufs=1))
        ps = ctx.enter_context(tc.psum_pool(name="ps", bufs=1))
        ctx.enter_context(tc.manual_schedule())

        def stage_scales(staged, first, scales):
            passes = scales.shape[0]
            nc.sync.dma_start(out=staged[4:P:8, first:first + passes, :].bitcast(I32),
                              in_=scales.rearrange("z q c -> q z c").bitcast(I32))

        def spread_scales(planes, staged):
            for r in range(4):
                nc.sync.dma_start(out=planes[r:P:32, :, :].rearrange("q z c -> q (z c)").bitcast(I32),
                                  in_=staged[8 * r + 4:P:32, :, :].rearrange("q z c -> q (z c)").bitcast(I32))

        def load_words(name, words, dtype):
            tile = sb.tile(list(words.shape[:2]) + [words.shape[2] // (4 if dtype == U32 else 1)], dtype, name=name,
                           align_bytes=64)
            nc.sync.dma_start(out=tile[:].bitcast(I32), in_=words.bitcast(I32))
            return tile

        wa_s_raw = sb.tile([P, 2, R], U8, name="wa_s_raw", align_bytes=64)
        nc.gpsimd.memset(wa_s_raw[:].rearrange("p z c -> p (z c)").bitcast(I32), 0)
        xt_s = sb.tile([P, 2, 512], U8, name="xt_s", align_bytes=64)
        nc.vector.memset(xt_s[:].rearrange("p z c -> p (z c)").bitcast(I32), 0)
        probe_in = sb.tile([P, 1], F32, name="probe_in")
        nc.vector.memset(probe_in[:], 0.0)
        table_probe = sb.tile([P, 1], F32, name="table_probe")
        nc.scalar.activation(out=table_probe[:], in_=probe_in[:], func=ACT.Tanh)
        planes2 = sb.tile([P, 5, 512], U8, name="planes2", align_bytes=64)
        nc.vector.memset(planes2[:].rearrange("p z c -> p (z c)").bitcast(I32), 0)
        xq_s, wq_s, wb_s = planes2[:, 0:2, :], planes2[:, 2:4, :], planes2[:, 4:5, :]

        def load_scale_rows(plane, scales, r):
            nc.sync.dma_start(out=plane[r:P:32, :, :].bitcast(I32),
                              in_=scales.rearrange("z (q r) c -> r q z c", r=4)[r].bitcast(I32))

        staged2 = sb.tile([P, 5, 512], U8, name="staged2", align_bytes=64)
        wa_raw = load_words("wa_raw", wa_words.rearrange("z p b -> p z b"), U8)
        for r in range(4):
            load_scale_rows(wa_s_raw, wa_scales, r)
        for r in range(2):
            load_scale_rows(xt_s, xt_scales, r)
        xt_c = load_words("xt_c", xt_words.rearrange("z p n t -> p z (n t)"), U32)
        for r in range(2, 4):
            load_scale_rows(xt_s, xt_scales, r)
        stage_scales(staged2, 0, xq_scales)
        stage_scales(staged2, 2, wq_scales)
        stage_scales(staged2, 4, wb_scales)
        wq_c = load_words("wq_c", wq_words.rearrange("z p n t -> p z (n t)"), U32)
        xq_c = load_words("xq_c", xq_words.rearrange("z p b -> p z b"), U8)
        spread_scales(planes2, staged2)
        wb_c = load_words("wb_c", wb_words.rearrange("z p n t -> p z (n t)"), U32)
        tg_t = {}
        for h in range(2):
            for pair in range(2):
                part = sb.tile([P, 2, HALF], F32, name="tg%d_%d" % (h, pair))
                nc.sync.dma_start(out=part[:], in_=tg[2 * pair * P:(2 * pair + 2) * P, h * HALF:(h + 1) * HALF]
                                  .rearrange("(i p) t -> p i t", p=P))
                tg_t[(h, 2 * pair)] = part[:, 0, :]
                tg_t[(h, 2 * pair + 1)] = part[:, 1, :]

        wa_s = sb.tile([P, 2, R], U8, name="wa_s", align_bytes=64)
        wa_c = [sb.tile([P, 2 * R], U8, name="wa_c%d" % z, align_bytes=64) for z in range(2)]

        def gather_code_columns(z):
            nc.vector.tensor_copy(out=wa_c[z][:].rearrange("p (j m b) -> p j m b", j=4, b=2),
                                  in_=wa_raw[:, z, :].rearrange("p (m j b) -> p j m b", j=4, b=2))

        gather_code_columns(0)
        nc.vector.tensor_copy(out=wa_s[:].rearrange("p z (j m) -> p z j m", j=4),
                              in_=wa_s_raw[:].rearrange("p z (m j) -> p z j m", j=4))
        gather_code_columns(1)

        hid_c = sb.tile([P, T], U32, name="hid_c", align_bytes=64)
        hid_s = sb.tile([P, T], U8, name="hid_s", align_bytes=64)
        pre = [ps.tile([P, 4, P], F32, name="pre%d" % c, tag="chunk%d" % c) for c in range(CHUNKS)]
        hid_in = [sb.tile([P, P * 4], BF16, name="hid_in%d" % c, align_bytes=64) for c in range(CHUNKS)]

        def first_layer_pass(c, z):
            cols = slice(c * P, (c + 1) * P)
            for j in range(4):
                nc.tensor.matmul_mx(out=pre[c][:, j, :], lhsT=wa_c[z][:, j * 2 * P:(j + 1) * 2 * P].bitcast(FP4X4),
                                    lhsT_scale=wa_s[:, z, j * P:(j + 1) * P],
                                    rhs=xt_c[:, z, cols].bitcast(FP8X4),
                                    rhs_scale=xt_s[:, z, cols],
                                    start=(z == 0 and j == 0), stop=(z == 1 and j == 3))

        def relu_out(c):
            src = pre[c][:].rearrange("p j t -> p t j")
            dst = hid_in[c][:].rearrange("p (t j) -> p t j", j=4)
            if c % 2 == 0:
                nc.scalar.activation(out=dst, in_=src, func=ACT.Relu)
            else:
                nc.vector.tensor_scalar(out=dst, in0=src, scalar1=0.0, scalar2=None, op0=ALU.max)

        def quantize_chunk(c):
            cols = slice(c * P, (c + 1) * P)
            nc.vector.quantize_mx(out=hid_c[:, cols].bitcast(FP8X4), scales=hid_s[:, cols], in_=hid_in[c][:])

        for first in (0, 2):
            for z in range(2):
                first_layer_pass(first, z)
                first_layer_pass(first + 1, z)
            relu_out(first)
            relu_out(first + 1)
            quantize_chunk(first)
            quantize_chunk(first + 1)

        pieces = [(i, 0, HALF) for i in range(4)] + [(i, HALF, T) for i in range(3)]
        pieces = pieces + [(3, HALF, HALF + P), (3, HALF + P, T)]
        banks = ["sum%d" % i for i in range(4)] + ["chunk%d" % c for c in range(CHUNKS)]

        def second_input_passes(k):
            i, t0, t1 = pieces[k]
            rows = slice(i * P, (i + 1) * P)
            total = ps.tile([P, t1 - t0], F32, name="total%d" % k, tag=banks[k % len(banks)])
            for z in range(2):
                for c0 in range(t0, t1, P):
                    nc.tensor.matmul_mx(out=total[:, c0 - t0:c0 - t0 + P], lhsT=wq_c[:, z, rows].bitcast(FP8X4),
                                        lhsT_scale=wq_s[:, z, rows],
                                        rhs=xq_c[:, z, 2 * c0:2 * (c0 + P)].bitcast(FP4X4),
                                        rhs_scale=xq_s[:, z, c0:c0 + P], start=(z == 0 and c0 == t0), stop=False)
            return total

        def finish(k, total):
            i, t0, t1 = pieces[k]
            rows = slice(i * P, (i + 1) * P)
            nc.tensor.matmul_mx(out=total[:], lhsT=wb_c[:, 0, rows].bitcast(FP8X4), lhsT_scale=wb_s[:, 0, rows],
                                rhs=hid_c[:, t0:t1].bitcast(FP8X4), rhs_scale=hid_s[:, t0:t1], start=False, stop=True)
            h = t0 // HALF
            rest = sb.tile([P, t1 - t0], F32, name="rest%d" % k)
            nc.vector.tensor_tensor(out=rest[:], in0=tg_t[(h, i)][:, t0 - h * HALF:t1 - h * HALF], in1=total[:],
                                    op=ALU.subtract)
            result = sb.tile([P, t1 - t0], F32, name="result%d" % k)
            nc.scalar.activation(out=result[:], in_=rest[:], func=ACT.Tanh)
            nc.sync.dma_start(out=out[rows, t0:t1], in_=result[:])

        leading = [second_input_passes(0), second_input_passes(1)]
        finish(0, leading[0])
        finish(1, leading[1])
        for k in range(2, len(pieces)):
            finish(k, second_input_passes(k))
